import numpy as np
import ml_dtypes


def mxq(x, axis, fmt="e4m3"):
    dtype, down = {"e4m3": (ml_dtypes.float8_e4m3fn, 7), "e5m2": (ml_dtypes.float8_e5m2, 14)}[fmt]
    v = np.moveaxis(np.asarray(x, np.float32).astype(ml_dtypes.bfloat16).astype(np.float64), axis, -1)
    blocks = v.reshape(v.shape[:-1] + (-1, 32))
    amax = np.abs(blocks).max(-1, keepdims=True)
    byte = np.maximum(np.where(amax > 0, np.frexp(amax)[1] - 1 + 127, 0) - down, 1)
    scale = np.exp2(byte - 127.0)
    codes = (blocks / scale).astype(np.float32).astype(dtype).astype(np.float64)
    return np.moveaxis((codes * scale).reshape(v.shape), -1, axis)


WIDE = False


def mx_kscale(k):
    if not WIDE:
        return np.ones(k)
    levels = np.array([10, -10, 5, -5, 0])
    if k % 512:
        return np.exp2(np.random.permutation(np.resize(levels, k // 32))).repeat(32)
    a = np.empty((k // 512, 16))
    for p in range(k // 512):
        a[p, :8] = np.random.permutation(np.resize(levels, 8))
        for g in range(8):
            far = levels[np.abs(levels - a[p, g]) >= 10]
            a[p, g + 8] = far[np.random.randint(len(far))]
    return np.exp2(a.ravel()).repeat(32)


def f64(x):
    return np.asarray(x).astype(np.float64)


def striped(idx):
    return np.tile(idx.reshape(-1, 16).T, (8, 1)).astype(np.uint16)


def unstriped(offs):
    return offs[:16].T.reshape(-1).astype(np.int64)


def pack_weight(w):
    k, n = w.shape
    w = f64(np.asarray(w, np.float32).astype(ml_dtypes.bfloat16)).reshape(k // 32, 32, n)
    amax = np.abs(w).max(1)
    byte = np.clip(np.where(amax > 0, np.frexp(amax)[1] - 1 + 127 - 7, 1), 1, 254)
    scaled = (w * np.exp2(127.0 - byte)[:, None, :]).reshape(k, n).astype(np.float32)
    words = np.ascontiguousarray(scaled.reshape(k // 512, 128, 4, n).transpose(0, 1, 3, 2)).astype(ml_dtypes.float8_e4m3fn).view(np.uint8)
    return words, np.ascontiguousarray(byte.astype(np.uint8).reshape(k // 512, 16, n))


def unpack_weight(words, scales):
    g, p, n, _ = words.shape
    vals = np.ascontiguousarray(words).view(ml_dtypes.float8_e4m3fn).astype(np.float64) * np.repeat(np.exp2(scales.astype(np.float64) - 127.0), 8, axis=1)[..., None]
    return vals.transpose(0, 1, 3, 2).reshape(g * 512, n)


E2M1 = np.array([0.0, 0.5, 1.0, 1.5, 2.0, 3.0, 4.0, 6.0, -0.0, -0.5, -1.0, -1.5, -2.0, -3.0, -4.0, -6.0])


def pack_fp4(w):
    k, n = w.shape
    w = f64(np.asarray(w, np.float32).astype(ml_dtypes.bfloat16)).reshape(k // 32, 32, n)
    amax = np.abs(w).max(1)
    mant, ex = np.frexp(amax / 6.0)
    byte = np.clip(np.where(amax > 0, np.where(mant > 0.5, ex, ex - 1) + 127, 1), 1, 254)
    scaled = (w * np.exp2(127.0 - byte)[:, None, :]).reshape(k, n).astype(np.float32)
    c = np.ascontiguousarray(scaled.reshape(k // 512, 128, 4, n).transpose(0, 1, 3, 2)).astype(ml_dtypes.float4_e2m1fn).view(np.uint8) & 0xF
    words = (c[..., 0::2] | (c[..., 1::2] << 4)).reshape(k // 512, 128, 2 * n)
    return np.ascontiguousarray(words), np.ascontiguousarray(byte.astype(np.uint8).reshape(k // 512, 16, n))


def unpack_fp4(words, scales):
    g, _, n = scales.shape
    words = np.ascontiguousarray(words).reshape(g, 128, n, 2)
    nib = np.empty((g, 128, n, 4), np.uint8)
    nib[..., 0::2] = words & 0xF
    nib[..., 1::2] = words >> 4
    vals = E2M1[nib] * np.repeat(np.exp2(scales.astype(np.float64) - 127.0), 8, axis=1)[..., None]
    return vals.transpose(0, 1, 3, 2).reshape(g * 512, n)


def relu(v):
    return np.maximum(v, 0.0)


K, T, S, H, N = 512, 4096, 1024, 512, 256


def setup_inputs():
    n = np.random.standard_normal
    s = mx_kscale(K)[:, None]
    u = mx_kscale(H)
    packed_xT = pack_weight(n((K, T)) * s)
    packed_w2 = pack_fp4(n((H, N)) / np.sqrt(H) / u[:, None])
    return {
        "x_words": packed_xT[0],
        "x_scales": packed_xT[1],
        "w1": (n((K, H)) / np.sqrt(K) / s).astype(np.float32),
        "w2_words": packed_w2[0],
        "w2_scales": packed_w2[1],
        "gamma": (np.random.uniform(0.5, 1.5, (H, 1)) * u[:, None]).astype(np.float32),
        "offs": striped(np.random.permutation(T)[:S]),
    }


def reference(x_words, x_scales, w1, w2_words, w2_scales, gamma, offs):
    xq = unpack_weight(x_words, x_scales)[:, unstriped(offs)]
    h = mxq(f64(w1), 0, "e4m3").T @ xq
    hn = (h - h.mean(axis=1, keepdims=True)) / np.sqrt(h.var(axis=1, keepdims=True) + 1e-5)
    z = relu(f64(gamma) * hn)
    return unpack_fp4(w2_words, w2_scales).T @ mxq(z, 0, "e4m3")

@@ -1,0 +1,230 @@
+from contextlib import ExitStack
+
+import concourse.mybir as mybir
+
+K, T, S, H, N = 512, 4096, 1024, 512, 256
+FLOPS = 2 * K * H * S + 2 * H * N * S
+EPS = 1e-5
+
+F32 = mybir.dt.float32
+BF16 = mybir.dt.bfloat16
+I32 = mybir.dt.int32
+U32 = mybir.dt.uint32
+U16 = mybir.dt.uint16
+U8 = mybir.dt.uint8
+FP8X4 = mybir.dt.float8_e4m3fn_x4
+FP4X4 = mybir.dt.float4_e2m1fn_x4
+ACT = mybir.ActivationFunctionType
+ALU = mybir.AluOpType
+
+P = 128
+PACK = 4
+HALF = 512
+CHUNK = 256
+
+
+def tile_picked_inorm_relu_p_kernel(
+    tc, x_words, x_scales, w1, w2_words, w2_scales, gamma, offs, out
+):
+    nc = tc.nc
+    with ExitStack() as ctx:
+        keep = ctx.enter_context(tc.tile_pool(name="keep", bufs=1))
+        ring = ctx.enter_context(tc.tile_pool(name="ring", bufs=4))
+        psum = ctx.enter_context(tc.psum_pool(name="psum", bufs=8))
+
+        offsets = keep.tile([P, S // 16], U16, name="offsets")
+        nc.sync.dma_start(offsets[:], offs)
+        w1_raw = keep.tile([P, PACK, H], F32, name="w1_raw")
+        w1_rows = w1.rearrange("(p j) c -> p j c", j=PACK)
+        nc.sync.dma_start(w1_raw[:, 0:2, :], w1_rows[:, 0:2, :])
+        scale_table = keep.tile([P, T], U8, name="scale_table", align_bytes=64)
+        nc.vector.memset(scale_table[:].bitcast(I32), 0)
+        nc.sync.dma_start(scale_table[:].bitcast(I32)[4:P:8, :], x_scales[0].bitcast(I32))
+        nc.sync.dma_start(w1_raw[:, 2:4, :], w1_rows[:, 2:4, :])
+        word_table = keep.tile([P, T], U32, name="word_table", align_bytes=64)
+        nc.sync.dma_start(word_table[:].bitcast(I32), x_words[0].rearrange("p n t -> p (n t)").bitcast(I32))
+        gam = keep.tile([P, PACK], F32, name="gam")
+        nc.sync.dma_start(gam[:], gamma.rearrange("(p t) o -> p (t o)", t=PACK))
+        w2_codes = keep.tile([P, 2 * N], U8, name="w2_codes", align_bytes=64)
+        nc.sync.dma_start(w2_codes[:].bitcast(I32), w2_words[0].bitcast(I32))
+
+        warm = keep.tile([P, 2], F32, name="warm")
+        nc.vector.memset(warm[:, 0:1], 1.0)
+        nc.scalar.activation(warm[:, 1:2], warm[:, 0:1], ACT.Abs_reciprocal_sqrt)
+
+        w2_plane = keep.tile([P, N], U8, name="w2_plane", align_bytes=64)
+        nc.gpsimd.memset(w2_plane[:].bitcast(I32), 0)
+        for q in range(4):
+            nc.gpsimd.dma_start(
+                w2_plane[:].bitcast(I32)[32 * q : 32 * q + 4, :], w2_scales[0].bitcast(I32)[4 * q : 4 * q + 4, :]
+            )
+
+        x_plane = keep.tile([P, S], U8, name="x_plane", align_bytes=64)
+        nc.vector.memset(x_plane[:].bitcast(I32), 0)
+        stats = keep.tile([P, PACK, 12], F32, name="stats")
+        nc.vector.memset(stats[:], float(HALF))
+
+        picked_scales = keep.tile([P, S], U8, name="picked_scales", align_bytes=64)
+        nc.vector.tensor_copy(picked_scales[:], scale_table[:].indirect(offsets[:]))
+
+        w1_bf = keep.tile([P, PACK * H], BF16, name="w1_bf", align_bytes=64)
+        w1_dst = w1_bf[:].rearrange("p (t m j) -> p m j t", t=PACK, j=PACK)
+        w1_src = w1_raw[:].rearrange("p j (m t) -> p m j t", t=PACK)
+        nc.scalar.copy(w1_dst[:, 64:128], w1_src[:, 64:128])
+        nc.vector.tensor_copy(w1_dst[:, 0:64], w1_src[:, 0:64])
+
+        for q in range(4):
+            nc.scalar.dma_start(
+                x_plane[:].bitcast(I32)[32 * q : 32 * q + 4, :],
+                picked_scales[:].bitcast(I32)[32 * q + 4 : 32 * q + 32 : 8, :],
+            )
+
+        w1_codes = keep.tile([P, H], U32, name="w1_codes", align_bytes=64)
+        w1_plane = keep.tile([P, H], U8, name="w1_plane", align_bytes=64)
+        nc.vector.quantize_mx(out=w1_codes[:].bitcast(FP8X4), scales=w1_plane[:], in_=w1_bf[:])
+
+        factors = keep.tile([P, PACK, 4], F32, name="factors")
+        nc.vector.tensor_copy(factors[:, :, 0], gam[:])
+        nc.vector.tensor_scalar(factors[:, :, 2], gam[:], float(HALF), None, ALU.mult)
+
+        picked_words = []
+        for half in range(2):
+            words = keep.tile([P, HALF], U32, name="picked_words%d" % half, align_bytes=64)
+            cols = slice(half * HALF // 16, (half + 1) * HALF // 16)
+            nc.vector.tensor_copy(words[:], word_table[:].indirect(offsets[:, cols]))
+            picked_words.append(words)
+
+        moments = keep.tile([P, PACK, 2], F32, name="moments")
+        rstd = keep.tile([P, PACK], F32, name="rstd")
+        affine = keep.tile([P, PACK, 4], F32, name="affine")
+        z_planes = [keep.tile([P, PACK, HALF], BF16, name="z_planes%d" % half, align_bytes=64) for half in range(2)]
+        squares = keep.tile([P, HALF], BF16, name="squares")
+
+        banks = {}
+        shrunk = {}
+
+        def first_product(t, half):
+            bank = psum.tile([P, HALF], F32, name="bank")
+            cols = slice(t * P, (t + 1) * P)
+            nc.tensor.matmul_mx(
+                out=bank[:],
+                lhsT=w1_codes[:, cols].bitcast(FP8X4),
+                lhsT_scale=w1_plane[:, cols],
+                rhs=picked_words[half][:].bitcast(FP8X4),
+                rhs_scale=x_plane[:, half * HALF : (half + 1) * HALF],
+                start=True,
+                stop=True,
+            )
+            banks[t, half] = bank
+
+        def scalar_mean(t):
+            h_small = keep.tile([P, HALF], F32, name="h_small%d" % t)
+            nc.scalar.activation(h_small[:], banks[t, 0][:], ACT.Identity, scale=1.0 / HALF, accum_out=stats[:, t, 4:5])
+            shrunk[t] = h_small
+
+        def scalar_spread(t):
+            nc.scalar.activation(
+                squares[:], banks[t, 0][:], ACT.Square, bias=stats[:, t, 4:5], scale=-1.0, accum_out=stats[:, t, 5:6]
+            )
+
+        def vector_stats(t, half):
+            nc.vector.bn_stats(stats[:, t, 6 * half : 6 * half + 6], banks[t, half][:])
+
+        def aggregate(t):
+            first = 3 if t in shrunk else 0
+            nc.vector.bn_aggr(moments[:, t, :], stats[:, t, first:12])
+            nc.scalar.activation(rstd[:, t : t + 1], moments[:, t, 1:2], ACT.Abs_reciprocal_sqrt, bias=EPS)
+
+        def coefficients(t):
+            nc.vector.tensor_scalar(factors[:, t, 1:2], moments[:, t, 0:1], gam[:, t : t + 1], -1.0, ALU.mult, ALU.mult)
+            nc.scalar.activation(affine[:, t, 0:3], factors[:, t, 0:3], ACT.Copy, scale=rstd[:, t : t + 1])
+
+        def vector_normalise(t):
+            source, column = (shrunk[t], 2) if t in shrunk else (banks[t, 0], 0)
+            nc.vector.tensor_scalar(
+                z_planes[0][:, t, :], source[:], affine[:, t, column : column + 1], affine[:, t, 1:2], ALU.mult, ALU.add
+            )
+
+        def scalar_normalise(t, half):
+            nc.scalar.activation(
+                z_planes[half][:, t, :], banks[t, half][:], ACT.Relu, bias=affine[:, t, 1:2], scale=affine[:, t, 0:1]
+            )
+
+        for t, half in [(0, 0), (1, 0), (0, 1), (1, 1), (2, 0), (2, 1), (3, 0), (3, 1)]:
+            first_product(t, half)
+        scalar_mean(0)
+        vector_stats(1, 0)
+        scalar_spread(0)
+        vector_stats(0, 1)
+        scalar_mean(2)
+        aggregate(0)
+        coefficients(0)
+        vector_stats(1, 1)
+        aggregate(1)
+        coefficients(1)
+        scalar_spread(2)
+        vector_stats(2, 1)
+        scalar_normalise(0, 1)
+        vector_stats(3, 0)
+        aggregate(2)
+        coefficients(2)
+        scalar_normalise(1, 0)
+        vector_stats(3, 1)
+        aggregate(3)
+        coefficients(3)
+        scalar_normalise(1, 1)
+        vector_normalise(0)
+        vector_normalise(2)
+        scalar_normalise(2, 1)
+        vector_normalise(3)
+        scalar_normalise(3, 1)
+
+        out_view = out.rearrange("(a p) n -> p a n", p=P)
+        woven = {}
+
+        def weave(c):
+            half, start = divmod(c * CHUNK, HALF)
+            z_bf = ring.tile([P, CHUNK * PACK], BF16, name="z_bf", align_bytes=64)
+            dst = z_bf[:].rearrange("p (g i t) -> p g t i", i=4, t=PACK)
+            src = z_planes[half][:, :, start : start + CHUNK].rearrange("p t (g i) -> p g t i", i=4)
+            if half == 0:
+                nc.vector.tensor_scalar(dst, src, 0.0, None, ALU.max)
+            elif c == 2:
+                nc.vector.tensor_copy(dst, src)
+            else:
+                nc.scalar.copy(dst, src)
+            woven[c] = z_bf
+
+        def second_product(c):
+            z_codes = ring.tile([P, CHUNK], U32, name="z_codes", align_bytes=64)
+            z_plane = ring.tile([P, CHUNK], U8, name="z_plane", align_bytes=64)
+            nc.vector.quantize_mx(out=z_codes[:].bitcast(FP8X4), scales=z_plane[:], in_=woven[c][:])
+            result = ring.tile([P, 2, CHUNK], F32, name="result")
+            last = c == S // CHUNK - 1
+            shared = None if last else psum.tile([P, 2, CHUNK], F32, name="bank")
+            for a in range(2):
+                sums = psum.tile([P, CHUNK], F32, name="bank")[:] if last else shared[:, a, :]
+                nc.tensor.matmul_mx(
+                    out=sums,
+                    lhsT=w2_codes[:, 2 * P * a : 2 * P * (a + 1)].bitcast(FP4X4),
+                    lhsT_scale=w2_plane[:, P * a : P * (a + 1)],
+                    rhs=z_codes[:].bitcast(FP8X4),
+                    rhs_scale=z_plane[:],
+                    start=True,
+                    stop=True,
+                )
+                if last and a == 0:
+                    nc.scalar.copy(result[:, a, :], sums)
+                elif last:
+                    nc.vector.tensor_copy(result[:, a, :], sums)
+            if not last:
+                nc.scalar.copy(result[:], shared[:])
+            nc.sync.dma_start(out_view[:, :, c * CHUNK : (c + 1) * CHUNK], result[:])
+
+        weave(0)
+        weave(1)
+        weave(3)
+        second_product(0)
+        weave(2)
+        for c in range(1, 4):
+            second_product(c)

@@ -29,14 +29,13 @@ def tile_picked_inorm_relu_p_kernel(
     nc = tc.nc
     with ExitStack() as ctx:
         keep = ctx.enter_context(tc.tile_pool(name="keep", bufs=1))
-        ring = ctx.enter_context(tc.tile_pool(name="ring", bufs=4))
-        psum = ctx.enter_context(tc.psum_pool(name="psum", bufs=8))
+        psum = ctx.enter_context(tc.psum_pool(name="psum", bufs=1))
 
         offsets = keep.tile([P, S // 16], U16, name="offsets")
-        nc.sync.dma_start(offsets[:], offs)
         w1_raw = keep.tile([P, PACK, H], F32, name="w1_raw")
         w1_rows = w1.rearrange("(p j) c -> p j c", j=PACK)
         nc.sync.dma_start(w1_raw[:, 0:2, :], w1_rows[:, 0:2, :])
+        nc.sync.dma_start(offsets[:], offs)
         scale_table = keep.tile([P, T], U8, name="scale_table", align_bytes=64)
         nc.vector.memset(scale_table[:].bitcast(I32), 0)
         nc.sync.dma_start(scale_table[:].bitcast(I32)[4:P:8, :], x_scales[0].bitcast(I32))
@@ -53,7 +52,7 @@ def tile_picked_inorm_relu_p_kernel(
         nc.scalar.activation(warm[:, 1:2], warm[:, 0:1], ACT.Abs_reciprocal_sqrt)
 
         w2_plane = keep.tile([P, N], U8, name="w2_plane", align_bytes=64)
-        nc.gpsimd.memset(w2_plane[:].bitcast(I32), 0)
+        nc.vector.memset(w2_plane[:].bitcast(I32), 0)
         for q in range(4):
             nc.gpsimd.dma_start(
                 w2_plane[:].bitcast(I32)[32 * q : 32 * q + 4, :], w2_scales[0].bitcast(I32)[4 * q : 4 * q + 4, :]
@@ -63,6 +62,9 @@ def tile_picked_inorm_relu_p_kernel(
         nc.vector.memset(x_plane[:].bitcast(I32), 0)
         stats = keep.tile([P, PACK, 12], F32, name="stats")
         nc.vector.memset(stats[:], float(HALF))
+        moments = keep.tile([P, PACK, 4], F32, name="moments")
+        nc.vector.memset(moments[:, :, 0:1], -float(HALF))
+        nc.vector.memset(moments[:, :, 1:2], -1.0)
 
         picked_scales = keep.tile([P, S], U8, name="picked_scales", align_bytes=64)
         nc.vector.tensor_copy(picked_scales[:], scale_table[:].indirect(offsets[:]))
@@ -83,9 +85,23 @@ def tile_picked_inorm_relu_p_kernel(
         w1_plane = keep.tile([P, H], U8, name="w1_plane", align_bytes=64)
         nc.vector.quantize_mx(out=w1_codes[:].bitcast(FP8X4), scales=w1_plane[:], in_=w1_bf[:])
 
-        factors = keep.tile([P, PACK, 4], F32, name="factors")
-        nc.vector.tensor_copy(factors[:, :, 0], gam[:])
-        nc.vector.tensor_scalar(factors[:, :, 2], gam[:], float(HALF), None, ALU.mult)
+        neg_gam = keep.tile([P, PACK], F32, name="neg_gam")
+        nc.vector.tensor_scalar(neg_gam[:], gam[:], -1.0, None, ALU.mult)
+
+        def keep_clock(bank_name, passes):
+            idle = psum.tile([32, H], F32, name=bank_name)
+            for step in range(passes):
+                nc.tensor.matmul_mx(
+                    out=idle[:],
+                    lhsT=w1_codes[:, 0:32].bitcast(FP8X4),
+                    lhsT_scale=w1_plane[:, 0:32],
+                    rhs=w1_codes[:].bitcast(FP8X4),
+                    rhs_scale=w1_plane[:],
+                    start=True,
+                    stop=True,
+                )
+
+        keep_clock("bank31", 3)
 
         picked_words = []
         for half in range(2):
@@ -94,7 +110,6 @@ def tile_picked_inorm_relu_p_kernel(
             nc.vector.tensor_copy(words[:], word_table[:].indirect(offsets[:, cols]))
             picked_words.append(words)
 
-        moments = keep.tile([P, PACK, 2], F32, name="moments")
         rstd = keep.tile([P, PACK], F32, name="rstd")
         affine = keep.tile([P, PACK, 4], F32, name="affine")
         z_planes = [keep.tile([P, PACK, HALF], BF16, name="z_planes%d" % half, align_bytes=64) for half in range(2)]
@@ -104,7 +119,7 @@ def tile_picked_inorm_relu_p_kernel(
         shrunk = {}
 
         def first_product(t, half):
-            bank = psum.tile([P, HALF], F32, name="bank")
+            bank = psum.tile([P, HALF], F32, name="bank%d%d" % (t, half))
             cols = slice(t * P, (t + 1) * P)
             nc.tensor.matmul_mx(
                 out=bank[:],
@@ -132,80 +147,82 @@ def tile_picked_inorm_relu_p_kernel(
 
         def aggregate(t):
             first = 3 if t in shrunk else 0
-            nc.vector.bn_aggr(moments[:, t, :], stats[:, t, first:12])
-            nc.scalar.activation(rstd[:, t : t + 1], moments[:, t, 1:2], ACT.Abs_reciprocal_sqrt, bias=EPS)
+            nc.vector.bn_aggr(moments[:, t, 2:4], stats[:, t, first:12])
+            nc.scalar.activation(rstd[:, t : t + 1], moments[:, t, 3:4], ACT.Abs_reciprocal_sqrt, bias=EPS)
 
         def coefficients(t):
-            nc.vector.tensor_scalar(factors[:, t, 1:2], moments[:, t, 0:1], gam[:, t : t + 1], -1.0, ALU.mult, ALU.mult)
-            nc.scalar.activation(affine[:, t, 0:3], factors[:, t, 0:3], ACT.Copy, scale=rstd[:, t : t + 1])
+            nc.vector.tensor_scalar(
+                affine[:, t, 0:3], moments[:, t, 0:3], rstd[:, t : t + 1], neg_gam[:, t : t + 1], ALU.mult, ALU.mult
+            )
 
         def vector_normalise(t):
-            source, column = (shrunk[t], 2) if t in shrunk else (banks[t, 0], 0)
+            source, column = (shrunk[t], 0) if t in shrunk else (banks[t, 0], 1)
             nc.vector.tensor_scalar(
-                z_planes[0][:, t, :], source[:], affine[:, t, column : column + 1], affine[:, t, 1:2], ALU.mult, ALU.add
+                z_planes[0][:, t, :], source[:], affine[:, t, column : column + 1], affine[:, t, 2:3], ALU.mult, ALU.add
             )
 
         def scalar_normalise(t, half):
             nc.scalar.activation(
-                z_planes[half][:, t, :], banks[t, half][:], ACT.Relu, bias=affine[:, t, 1:2], scale=affine[:, t, 0:1]
+                z_planes[half][:, t, :], banks[t, half][:], ACT.Relu, bias=affine[:, t, 2:3], scale=affine[:, t, 1:2]
             )
 
-        for t, half in [(0, 0), (1, 0), (0, 1), (1, 1), (2, 0), (2, 1), (3, 0), (3, 1)]:
+        for t, half in [(0, 0), (1, 0), (3, 0), (2, 0), (0, 1), (1, 1), (2, 1), (3, 1)]:
             first_product(t, half)
         scalar_mean(0)
-        vector_stats(1, 0)
+        scalar_mean(1)
+        vector_stats(3, 0)
         scalar_spread(0)
         vector_stats(0, 1)
-        scalar_mean(2)
-        aggregate(0)
-        coefficients(0)
+        scalar_spread(1)
         vector_stats(1, 1)
-        aggregate(1)
-        coefficients(1)
-        scalar_spread(2)
+        aggregate(0)
+        scalar_mean(2)
         vector_stats(2, 1)
-        scalar_normalise(0, 1)
-        vector_stats(3, 0)
-        aggregate(2)
-        coefficients(2)
-        scalar_normalise(1, 0)
+        coefficients(0)
+        aggregate(1)
+        scalar_spread(2)
         vector_stats(3, 1)
+        coefficients(1)
+        aggregate(2)
         aggregate(3)
+        scalar_normalise(0, 1)
+        vector_normalise(0)
+        coefficients(2)
         coefficients(3)
         scalar_normalise(1, 1)
-        vector_normalise(0)
+        vector_normalise(1)
+        vector_normalise(3)
         vector_normalise(2)
         scalar_normalise(2, 1)
-        vector_normalise(3)
         scalar_normalise(3, 1)
+
+        for bank_name in ("bank10", "bank20", "bank11", "bank31"):
+            keep_clock(bank_name, 2)
 
         out_view = out.rearrange("(a p) n -> p a n", p=P)
         woven = {}
 
-        def weave(c):
-            half, start = divmod(c * CHUNK, HALF)
-            z_bf = ring.tile([P, CHUNK * PACK], BF16, name="z_bf", align_bytes=64)
+        def weave(start, width, on_scalar):
+            half, first = divmod(start, HALF)
+            z_bf = keep.tile([P, width * PACK], BF16, name="z_bf%d" % start, align_bytes=64)
             dst = z_bf[:].rearrange("p (g i t) -> p g t i", i=4, t=PACK)
-            src = z_planes[half][:, :, start : start + CHUNK].rearrange("p t (g i) -> p g t i", i=4)
-            if half == 0:
-                nc.vector.tensor_scalar(dst, src, 0.0, None, ALU.max)
-            elif c == 2:
-                nc.vector.tensor_copy(dst, src)
-            else:
+            src = z_planes[half][:, :, first : first + width].rearrange("p t (g i) -> p g t i", i=4)
+            if on_scalar:
                 nc.scalar.copy(dst, src)
-            woven[c] = z_bf
+            elif half == 0:
+                nc.vector.tensor_scalar(dst, src, 0.0, None, ALU.max)
+            else:
+                nc.vector.tensor_copy(dst, src)
+            woven[start] = z_bf
 
-        def second_product(c):
-            z_codes = ring.tile([P, CHUNK], U32, name="z_codes", align_bytes=64)
-            z_plane = ring.tile([P, CHUNK], U8, name="z_plane", align_bytes=64)
-            nc.vector.quantize_mx(out=z_codes[:].bitcast(FP8X4), scales=z_plane[:], in_=woven[c][:])
-            result = ring.tile([P, 2, CHUNK], F32, name="result")
-            last = c == S // CHUNK - 1
-            shared = None if last else psum.tile([P, 2, CHUNK], F32, name="bank")
+        def second_product(start, width, bank_name):
+            z_codes = keep.tile([P, width], U32, name="z_codes%d" % start, align_bytes=64)
+            z_plane = keep.tile([P, width], U8, name="z_plane%d" % start, align_bytes=64)
+            nc.vector.quantize_mx(out=z_codes[:].bitcast(FP8X4), scales=z_plane[:], in_=woven[start][:])
+            bank = psum.tile([P, 2, width], F32, name=bank_name)
             for a in range(2):
-                sums = psum.tile([P, CHUNK], F32, name="bank")[:] if last else shared[:, a, :]
                 nc.tensor.matmul_mx(
-                    out=sums,
+                    out=bank[:, a, :],
                     lhsT=w2_codes[:, 2 * P * a : 2 * P * (a + 1)].bitcast(FP4X4),
                     lhsT_scale=w2_plane[:, P * a : P * (a + 1)],
                     rhs=z_codes[:].bitcast(FP8X4),
@@ -213,18 +230,25 @@ def tile_picked_inorm_relu_p_kernel(
                     start=True,
                     stop=True,
                 )
-                if last and a == 0:
-                    nc.scalar.copy(result[:, a, :], sums)
-                elif last:
-                    nc.vector.tensor_copy(result[:, a, :], sums)
-            if not last:
-                nc.scalar.copy(result[:], shared[:])
-            nc.sync.dma_start(out_view[:, :, c * CHUNK : (c + 1) * CHUNK], result[:])
+            return bank
 
-        weave(0)
-        weave(1)
-        weave(3)
-        second_product(0)
-        weave(2)
-        for c in range(1, 4):
-            second_product(c)
+        def whole_chunk(start, bank_name):
+            bank = second_product(start, CHUNK, bank_name)
+            result = keep.tile([P, 2, CHUNK], F32, name="result%d" % start)
+            nc.scalar.copy(result[:], bank[:])
+            nc.sync.dma_start(out_view[:, :, start : start + CHUNK], result[:])
+
+        weave(0, CHUNK, False)
+        weave(768, CHUNK, True)
+        weave(256, CHUNK, False)
+        whole_chunk(0, "bank00")
+        whole_chunk(768, "bank10")
+        whole_chunk(256, "bank20")
+        weave(512, 128, False)
+        weave(640, 128, False)
+        result = keep.tile([P, 2, CHUNK], F32, name="result512")
+        bank = second_product(512, 128, "bank01")
+        nc.scalar.copy(result[:, :, 0:128], bank[:])
+        bank = second_product(640, 128, "bank11")
+        nc.vector.tensor_copy(result[:, :, 128:256], bank[:])
+        nc.sync.dma_start(out_view[:, :, 512:768], result[:])

@@ -36,14 +36,16 @@ def tile_picked_inorm_relu_p_kernel(
         w1_rows = w1.rearrange("(p j) c -> p j c", j=PACK)
         nc.sync.dma_start(w1_raw[:, 0:2, :], w1_rows[:, 0:2, :])
         nc.sync.dma_start(offsets[:], offs)
+        gam = keep.tile([P, PACK], F32, name="gam")
+        nc.sync.dma_start(gam[:], gamma.rearrange("(p t) o -> p (t o)", t=PACK))
         scale_table = keep.tile([P, T], U8, name="scale_table", align_bytes=64)
         nc.vector.memset(scale_table[:].bitcast(I32), 0)
         nc.sync.dma_start(scale_table[:].bitcast(I32)[4:P:8, :], x_scales[0].bitcast(I32))
         nc.sync.dma_start(w1_raw[:, 2:4, :], w1_rows[:, 2:4, :])
         word_table = keep.tile([P, T], U32, name="word_table", align_bytes=64)
-        nc.sync.dma_start(word_table[:].bitcast(I32), x_words[0].rearrange("p n t -> p (n t)").bitcast(I32))
-        gam = keep.tile([P, PACK], F32, name="gam")
-        nc.sync.dma_start(gam[:], gamma.rearrange("(p t) o -> p (t o)", t=PACK))
+        nc.sync.dma_start(
+            word_table[:].bitcast(I32), x_words[0].rearrange("p n t -> p (n t)").bitcast(I32), max_dma_last_dim=8192
+        )
         w2_codes = keep.tile([P, 2 * N], U8, name="w2_codes", align_bytes=64)
         nc.sync.dma_start(w2_codes[:].bitcast(I32), w2_words[0].bitcast(I32))
 
@@ -72,8 +74,8 @@ def tile_picked_inorm_relu_p_kernel(
         w1_bf = keep.tile([P, PACK * H], BF16, name="w1_bf", align_bytes=64)
         w1_dst = w1_bf[:].rearrange("p (t m j) -> p m j t", t=PACK, j=PACK)
         w1_src = w1_raw[:].rearrange("p j (m t) -> p m j t", t=PACK)
-        nc.scalar.copy(w1_dst[:, 64:128], w1_src[:, 64:128])
-        nc.vector.tensor_copy(w1_dst[:, 0:64], w1_src[:, 0:64])
+        nc.scalar.copy(w1_dst[:, :, 0:2], w1_src[:, :, 0:2])
+        nc.vector.tensor_copy(w1_dst[:, :, 2:4], w1_src[:, :, 2:4])
 
         for q in range(4):
             nc.scalar.dma_start(

@@ -20,7 +20,6 @@ ALU = mybir.AluOpType
 P = 128
 PACK = 4
 HALF = 512
-CHUNK = 256
 
 
 def tile_picked_inorm_relu_p_kernel(
@@ -49,6 +48,7 @@ def tile_picked_inorm_relu_p_kernel(
         w2_codes = keep.tile([P, 2 * N], U8, name="w2_codes", align_bytes=64)
         nc.sync.dma_start(w2_codes[:].bitcast(I32), w2_words[0].bitcast(I32))
 
+
         warm = keep.tile([P, 2], F32, name="warm")
         nc.vector.memset(warm[:, 0:1], 1.0)
         nc.scalar.activation(warm[:, 1:2], warm[:, 0:1], ACT.Abs_reciprocal_sqrt)
@@ -70,13 +70,11 @@ def tile_picked_inorm_relu_p_kernel(
 
         picked_scales = keep.tile([P, S], U8, name="picked_scales", align_bytes=64)
         nc.vector.tensor_copy(picked_scales[:], scale_table[:].indirect(offsets[:]))
-
         w1_bf = keep.tile([P, PACK * H], BF16, name="w1_bf", align_bytes=64)
         w1_dst = w1_bf[:].rearrange("p (t m j) -> p m j t", t=PACK, j=PACK)
         w1_src = w1_raw[:].rearrange("p j (m t) -> p m j t", t=PACK)
         nc.scalar.copy(w1_dst[:, :, 0:2], w1_src[:, :, 0:2])
         nc.vector.tensor_copy(w1_dst[:, :, 2:4], w1_src[:, :, 2:4])
-
         for q in range(4):
             nc.scalar.dma_start(
                 x_plane[:].bitcast(I32)[32 * q : 32 * q + 4, :],
@@ -90,20 +88,17 @@ def tile_picked_inorm_relu_p_kernel(
         neg_gam = keep.tile([P, PACK], F32, name="neg_gam")
         nc.vector.tensor_scalar(neg_gam[:], gam[:], -1.0, None, ALU.mult)
 
-        def keep_clock(bank_name, passes):
-            idle = psum.tile([32, H], F32, name=bank_name)
-            for step in range(passes):
-                nc.tensor.matmul_mx(
-                    out=idle[:],
-                    lhsT=w1_codes[:, 0:32].bitcast(FP8X4),
-                    lhsT_scale=w1_plane[:, 0:32],
-                    rhs=w1_codes[:].bitcast(FP8X4),
-                    rhs_scale=w1_plane[:],
-                    start=True,
-                    stop=True,
-                )
-
-        keep_clock("bank31", 3)
+        idle = psum.tile([32, H], F32, name="bank31")
+        for step in range(2):
+            nc.tensor.matmul_mx(
+                out=idle[:],
+                lhsT=w1_codes[:, 0:32].bitcast(FP8X4),
+                lhsT_scale=w1_plane[:, 0:32],
+                rhs=w1_codes[:].bitcast(FP8X4),
+                rhs_scale=w1_plane[:],
+                start=True,
+                stop=True,
+            )
 
         picked_words = []
         for half in range(2):
@@ -112,6 +107,7 @@ def tile_picked_inorm_relu_p_kernel(
             nc.vector.tensor_copy(words[:], word_table[:].indirect(offsets[:, cols]))
             picked_words.append(words)
 
+
         rstd = keep.tile([P, PACK], F32, name="rstd")
         affine = keep.tile([P, PACK, 4], F32, name="affine")
         z_planes = [keep.tile([P, PACK, HALF], BF16, name="z_planes%d" % half, align_bytes=64) for half in range(2)]
@@ -119,6 +115,7 @@ def tile_picked_inorm_relu_p_kernel(
 
         banks = {}
         shrunk = {}
+        first_stat = {}
 
         def first_product(t, half):
             bank = psum.tile([P, HALF], F32, name="bank%d%d" % (t, half))
@@ -134,22 +131,28 @@ def tile_picked_inorm_relu_p_kernel(
             )
             banks[t, half] = bank
 
-        def scalar_mean(t):
-            h_small = keep.tile([P, HALF], F32, name="h_small%d" % t)
-            nc.scalar.activation(h_small[:], banks[t, 0][:], ACT.Identity, scale=1.0 / HALF, accum_out=stats[:, t, 4:5])
-            shrunk[t] = h_small
-
-        def scalar_spread(t):
+        def scalar_mean(t, half, at):
+            h_small = keep.tile([P, HALF], F32, name="h_small%d%d" % (t, half))
             nc.scalar.activation(
-                squares[:], banks[t, 0][:], ACT.Square, bias=stats[:, t, 4:5], scale=-1.0, accum_out=stats[:, t, 5:6]
+                h_small[:], banks[t, half][:], ACT.Identity, scale=1.0 / HALF, accum_out=stats[:, t, at + 1 : at + 2]
+            )
+            shrunk[t, half] = h_small
+
+        def scalar_spread(t, half, at):
+            nc.scalar.activation(
+                squares[:],
+                banks[t, half][:],
+                ACT.Square,
+                bias=stats[:, t, at + 1 : at + 2],
+                scale=-1.0,
+                accum_out=stats[:, t, at + 2 : at + 3],
             )
 
         def vector_stats(t, half):
             nc.vector.bn_stats(stats[:, t, 6 * half : 6 * half + 6], banks[t, half][:])
 
-        def aggregate(t):
-            first = 3 if t in shrunk else 0
-            nc.vector.bn_aggr(moments[:, t, 2:4], stats[:, t, first:12])
+        def aggregate(t, first, last):
+            nc.vector.bn_aggr(moments[:, t, 2:4], stats[:, t, first:last])
             nc.scalar.activation(rstd[:, t : t + 1], moments[:, t, 3:4], ACT.Abs_reciprocal_sqrt, bias=EPS)
 
         def coefficients(t):
@@ -157,52 +160,70 @@ def tile_picked_inorm_relu_p_kernel(
                 affine[:, t, 0:3], moments[:, t, 0:3], rstd[:, t : t + 1], neg_gam[:, t : t + 1], ALU.mult, ALU.mult
             )
 
-        def vector_normalise(t):
-            source, column = (shrunk[t], 0) if t in shrunk else (banks[t, 0], 1)
+        def vector_normalise(t, half, first=0, last=HALF):
+            source, column = (shrunk[t, half], 0) if (t, half) in shrunk else (banks[t, half], 1)
             nc.vector.tensor_scalar(
-                z_planes[0][:, t, :], source[:], affine[:, t, column : column + 1], affine[:, t, 2:3], ALU.mult, ALU.add
+                z_planes[half][:, t, first:last],
+                source[:, first:last],
+                affine[:, t, column : column + 1],
+                affine[:, t, 2:3],
+                ALU.mult,
+                ALU.add,
             )
 
-        def scalar_normalise(t, half):
+        def gpsimd_normalise(t, half, first=0, last=HALF):
+            nc.gpsimd.tensor_scalar(
+                z_planes[half][:, t, first:last],
+                shrunk[t, half][:, first:last],
+                affine[:, t, 0:1],
+                affine[:, t, 2:3],
+                ALU.mult,
+                ALU.add,
+            )
+
+        def scalar_normalise(t, half, first=0, last=HALF):
             nc.scalar.activation(
-                z_planes[half][:, t, :], banks[t, half][:], ACT.Relu, bias=affine[:, t, 2:3], scale=affine[:, t, 1:2]
+                z_planes[half][:, t, first:last],
+                banks[t, half][:, first:last],
+                ACT.Relu,
+                bias=affine[:, t, 2:3],
+                scale=affine[:, t, 1:2],
             )
 
-        for t, half in [(0, 0), (1, 0), (3, 0), (2, 0), (0, 1), (1, 1), (2, 1), (3, 1)]:
+        for t, half in [[0,0],[1,0],[3,0],[2,0],[0,1],[1,1],[2,1],[3,1]]:
             first_product(t, half)
-        scalar_mean(0)
-        scalar_mean(1)
+        scalar_mean(0, 0, 3)
+        scalar_mean(1, 0, 3)
         vector_stats(3, 0)
-        scalar_spread(0)
+        scalar_spread(0, 0, 3)
         vector_stats(0, 1)
-        scalar_spread(1)
+        scalar_spread(1, 0, 3)
         vector_stats(1, 1)
-        aggregate(0)
-        scalar_mean(2)
+        aggregate(0, 3, 12)
+        scalar_mean(2, 0, 3)
         vector_stats(2, 1)
         coefficients(0)
-        aggregate(1)
-        scalar_spread(2)
+        aggregate(1, 3, 12)
+        scalar_spread(2, 0, 3)
         vector_stats(3, 1)
         coefficients(1)
-        aggregate(2)
-        aggregate(3)
+        aggregate(2, 3, 12)
+        aggregate(3, 0, 12)
         scalar_normalise(0, 1)
-        vector_normalise(0)
+        vector_normalise(0, 0)
         coefficients(2)
         coefficients(3)
         scalar_normalise(1, 1)
-        vector_normalise(1)
-        vector_normalise(3)
-        vector_normalise(2)
+        vector_normalise(1, 0)
+        vector_normalise(3, 0)
+        vector_normalise(2, 0)
         scalar_normalise(2, 1)
         scalar_normalise(3, 1)
 
-        for bank_name in ("bank10", "bank20", "bank11", "bank31"):
-            keep_clock(bank_name, 2)
-
         out_view = out.rearrange("(a p) n -> p a n", p=P)
         woven = {}
+        products = {}
+        results = {}
 
         def weave(start, width, on_scalar):
             half, first = divmod(start, HALF)
@@ -232,25 +253,39 @@ def tile_picked_inorm_relu_p_kernel(
                     start=True,
                     stop=True,
                 )
-            return bank
+            products[start] = bank
 
-        def whole_chunk(start, bank_name):
-            bank = second_product(start, CHUNK, bank_name)
-            result = keep.tile([P, 2, CHUNK], F32, name="result%d" % start)
-            nc.scalar.copy(result[:], bank[:])
-            nc.sync.dma_start(out_view[:, :, start : start + CHUNK], result[:])
+        def empty(start, width, on_scalar, store_start, store_width):
+            if store_start not in results:
+                results[store_start] = keep.tile([P, 2, store_width], F32, name="result%d" % store_start)
+            dst = results[store_start][:, :, start - store_start : start - store_start + width]
+            if on_scalar:
+                nc.scalar.copy(dst, products[start][:])
+            else:
+                nc.vector.tensor_copy(dst, products[start][:])
 
-        weave(0, CHUNK, False)
-        weave(768, CHUNK, True)
-        weave(256, CHUNK, False)
-        whole_chunk(0, "bank00")
-        whole_chunk(768, "bank10")
-        whole_chunk(256, "bank20")
+        def store(start, width):
+            nc.sync.dma_start(out_view[:, :, start : start + width], results[start][:])
+
+        weave(0, 256, False)
+        weave(768, 256, True)
+        weave(256, 128, False)
+        second_product(0, 256, "bank00")
+        empty(0, 256, True, 0, 256)
+        store(0, 256)
+        weave(384, 128, False)
+        second_product(256, 128, "bank10")
+        second_product(768, 256, "bank20")
         weave(512, 128, False)
+        second_product(384, 128, "bank30")
+        empty(256, 128, True, 256, 256)
+        empty(768, 256, True, 768, 256)
+        store(768, 256)
+        empty(384, 128, True, 256, 256)
+        store(256, 256)
         weave(640, 128, False)
-        result = keep.tile([P, 2, CHUNK], F32, name="result512")
-        bank = second_product(512, 128, "bank01")
-        nc.scalar.copy(result[:, :, 0:128], bank[:])
-        bank = second_product(640, 128, "bank11")
-        nc.vector.tensor_copy(result[:, :, 128:256], bank[:])
-        nc.sync.dma_start(out_view[:, :, 512:768], result[:])
+        second_product(512, 128, "bank01")
+        second_product(640, 128, "bank11")
+        empty(512, 128, False, 512, 256)
+        empty(640, 128, False, 512, 256)
+        store(512, 256)

@@ -71,10 +71,10 @@ def tile_picked_inorm_relu_p_kernel(
         picked_scales = keep.tile([P, S], U8, name="picked_scales", align_bytes=64)
         nc.vector.tensor_copy(picked_scales[:], scale_table[:].indirect(offsets[:]))
         w1_bf = keep.tile([P, PACK * H], BF16, name="w1_bf", align_bytes=64)
-        w1_dst = w1_bf[:].rearrange("p (t m j) -> p m j t", t=PACK, j=PACK)
-        w1_src = w1_raw[:].rearrange("p j (m t) -> p m j t", t=PACK)
-        nc.scalar.copy(w1_dst[:, :, 0:2], w1_src[:, :, 0:2])
-        nc.vector.tensor_copy(w1_dst[:, :, 2:4], w1_src[:, :, 2:4])
+        w1_dst = w1_bf[:].rearrange("p (u e m j) -> p u m j e", u=2, e=2, j=PACK)
+        w1_src = w1_raw[:].rearrange("p j (m u e) -> p u m j e", u=2, e=2)
+        nc.scalar.copy(w1_dst[:, :, :, 0:2], w1_src[:, :, :, 0:2])
+        nc.vector.tensor_copy(w1_dst[:, :, :, 2:4], w1_src[:, :, :, 2:4])
         for q in range(4):
             nc.scalar.dma_start(
                 x_plane[:].bitcast(I32)[32 * q : 32 * q + 4, :],

@@ -95,7 +95,7 @@ def tile_picked_inorm_relu_p_kernel(
                 lhsT=w1_codes[:, 0:32].bitcast(FP8X4),
                 lhsT_scale=w1_plane[:, 0:32],
                 rhs=w1_codes[:].bitcast(FP8X4),
-                rhs_scale=w1_plane[:],
+                rhs_scale=x_plane[:, 0:H],
                 start=True,
                 stop=True,
             )
@@ -190,7 +190,7 @@ def tile_picked_inorm_relu_p_kernel(
                 scale=affine[:, t, 1:2],
             )
 
-        for t, half in [[0,0],[1,0],[3,0],[2,0],[0,1],[1,1],[2,1],[3,1]]:
+        for t, half in [[0,0],[3,0],[1,0],[0,1],[1,1],[2,0],[2,1],[3,1]]:
             first_product(t, half)
         scalar_mean(0, 0, 3)
         scalar_mean(1, 0, 3)

@@ -19,7 +19,12 @@ ALU = mybir.AluOpType
 
 P = 128
 PACK = 4
+QUADRANTS = 4
 HALF = 512
+WIDE = 256
+NARROW = 128
+VECTOR_SHARE = 84
+SCALAR_SLOTS = (0, 1, 2)
 
 
 def tile_picked_inorm_relu_p_kernel(
@@ -40,14 +45,13 @@ def tile_picked_inorm_relu_p_kernel(
         scale_table = keep.tile([P, T], U8, name="scale_table", align_bytes=64)
         nc.vector.memset(scale_table[:].bitcast(I32), 0)
         nc.sync.dma_start(scale_table[:].bitcast(I32)[4:P:8, :], x_scales[0].bitcast(I32))
-        nc.sync.dma_start(w1_raw[:, 2:4, :], w1_rows[:, 2:4, :])
         word_table = keep.tile([P, T], U32, name="word_table", align_bytes=64)
-        nc.sync.dma_start(
-            word_table[:].bitcast(I32), x_words[0].rearrange("p n t -> p (n t)").bitcast(I32), max_dma_last_dim=8192
-        )
+        x_flat = x_words[0].rearrange("p n t -> p (n t)").bitcast(I32)
+        nc.sync.dma_start(word_table[:].bitcast(I32)[:, 0 : T // 2], x_flat[:, 0 : T // 2])
+        nc.sync.dma_start(w1_raw[:, 2:4, :], w1_rows[:, 2:4, :])
+        nc.sync.dma_start(word_table[:].bitcast(I32)[:, T // 2 : T], x_flat[:, T // 2 : T])
         w2_codes = keep.tile([P, 2 * N], U8, name="w2_codes", align_bytes=64)
         nc.sync.dma_start(w2_codes[:].bitcast(I32), w2_words[0].bitcast(I32))
-
 
         warm = keep.tile([P, 2], F32, name="warm")
         nc.vector.memset(warm[:, 0:1], 1.0)
@@ -55,7 +59,7 @@ def tile_picked_inorm_relu_p_kernel(
 
         w2_plane = keep.tile([P, N], U8, name="w2_plane", align_bytes=64)
         nc.vector.memset(w2_plane[:].bitcast(I32), 0)
-        for q in range(4):
+        for q in range(QUADRANTS):
             nc.gpsimd.dma_start(
                 w2_plane[:].bitcast(I32)[32 * q : 32 * q + 4, :], w2_scales[0].bitcast(I32)[4 * q : 4 * q + 4, :]
             )
@@ -70,12 +74,15 @@ def tile_picked_inorm_relu_p_kernel(
 
         picked_scales = keep.tile([P, S], U8, name="picked_scales", align_bytes=64)
         nc.vector.tensor_copy(picked_scales[:], scale_table[:].indirect(offsets[:]))
+
         w1_bf = keep.tile([P, PACK * H], BF16, name="w1_bf", align_bytes=64)
         w1_dst = w1_bf[:].rearrange("p (u e m j) -> p u m j e", u=2, e=2, j=PACK)
         w1_src = w1_raw[:].rearrange("p j (m u e) -> p u m j e", u=2, e=2)
         nc.scalar.copy(w1_dst[:, :, :, 0:2], w1_src[:, :, :, 0:2])
-        nc.vector.tensor_copy(w1_dst[:, :, :, 2:4], w1_src[:, :, :, 2:4])
-        for q in range(4):
+        nc.vector.tensor_copy(w1_dst[:, :, 0:VECTOR_SHARE, 2:4], w1_src[:, :, 0:VECTOR_SHARE, 2:4])
+        nc.scalar.copy(w1_dst[:, :, VECTOR_SHARE:P, 2:4], w1_src[:, :, VECTOR_SHARE:P, 2:4])
+
+        for q in range(QUADRANTS):
             nc.scalar.dma_start(
                 x_plane[:].bitcast(I32)[32 * q : 32 * q + 4, :],
                 picked_scales[:].bitcast(I32)[32 * q + 4 : 32 * q + 32 : 8, :],
@@ -95,7 +102,7 @@ def tile_picked_inorm_relu_p_kernel(
                 lhsT=w1_codes[:, 0:32].bitcast(FP8X4),
                 lhsT_scale=w1_plane[:, 0:32],
                 rhs=w1_codes[:].bitcast(FP8X4),
-                rhs_scale=x_plane[:, 0:H],
+                rhs_scale=w1_plane[:],
                 start=True,
                 stop=True,
             )
@@ -107,15 +114,13 @@ def tile_picked_inorm_relu_p_kernel(
             nc.vector.tensor_copy(words[:], word_table[:].indirect(offsets[:, cols]))
             picked_words.append(words)
 
-
         rstd = keep.tile([P, PACK], F32, name="rstd")
         affine = keep.tile([P, PACK, 4], F32, name="affine")
-        z_planes = [keep.tile([P, PACK, HALF], BF16, name="z_planes%d" % half, align_bytes=64) for half in range(2)]
+        z_slots = [keep.tile([P, PACK, HALF], BF16, name="z_slots%d" % half, align_bytes=64) for half in range(2)]
         squares = keep.tile([P, HALF], BF16, name="squares")
 
         banks = {}
         shrunk = {}
-        first_stat = {}
 
         def first_product(t, half):
             bank = psum.tile([P, HALF], F32, name="bank%d%d" % (t, half))
@@ -131,28 +136,22 @@ def tile_picked_inorm_relu_p_kernel(
             )
             banks[t, half] = bank
 
-        def scalar_mean(t, half, at):
-            h_small = keep.tile([P, HALF], F32, name="h_small%d%d" % (t, half))
-            nc.scalar.activation(
-                h_small[:], banks[t, half][:], ACT.Identity, scale=1.0 / HALF, accum_out=stats[:, t, at + 1 : at + 2]
-            )
-            shrunk[t, half] = h_small
+        def scalar_mean(t):
+            h_small = keep.tile([P, HALF], F32, name="h_small%d" % t)
+            nc.scalar.activation(h_small[:], banks[t, 0][:], ACT.Identity, scale=1.0 / HALF, accum_out=stats[:, t, 4:5])
+            shrunk[t] = h_small
 
-        def scalar_spread(t, half, at):
+        def scalar_spread(t):
             nc.scalar.activation(
-                squares[:],
-                banks[t, half][:],
-                ACT.Square,
-                bias=stats[:, t, at + 1 : at + 2],
-                scale=-1.0,
-                accum_out=stats[:, t, at + 2 : at + 3],
+                squares[:], banks[t, 0][:], ACT.Square, bias=stats[:, t, 4:5], scale=-1.0, accum_out=stats[:, t, 5:6]
             )
 
         def vector_stats(t, half):
             nc.vector.bn_stats(stats[:, t, 6 * half : 6 * half + 6], banks[t, half][:])
 
-        def aggregate(t, first, last):
-            nc.vector.bn_aggr(moments[:, t, 2:4], stats[:, t, first:last])
+        def aggregate(t):
+            first = 3 if t in SCALAR_SLOTS else 0
+            nc.vector.bn_aggr(moments[:, t, 2:4], stats[:, t, first:12])
             nc.scalar.activation(rstd[:, t : t + 1], moments[:, t, 3:4], ACT.Abs_reciprocal_sqrt, bias=EPS)
 
         def coefficients(t):
@@ -160,65 +159,47 @@ def tile_picked_inorm_relu_p_kernel(
                 affine[:, t, 0:3], moments[:, t, 0:3], rstd[:, t : t + 1], neg_gam[:, t : t + 1], ALU.mult, ALU.mult
             )
 
-        def vector_normalise(t, half, first=0, last=HALF):
-            source, column = (shrunk[t, half], 0) if (t, half) in shrunk else (banks[t, half], 1)
+        def vector_normalise(t):
+            source, column = (shrunk[t], 0) if t in SCALAR_SLOTS else (banks[t, 0], 1)
             nc.vector.tensor_scalar(
-                z_planes[half][:, t, first:last],
-                source[:, first:last],
-                affine[:, t, column : column + 1],
-                affine[:, t, 2:3],
-                ALU.mult,
-                ALU.add,
+                z_slots[0][:, t, :], source[:], affine[:, t, column : column + 1], affine[:, t, 2:3], ALU.mult, ALU.add
             )
 
-        def gpsimd_normalise(t, half, first=0, last=HALF):
-            nc.gpsimd.tensor_scalar(
-                z_planes[half][:, t, first:last],
-                shrunk[t, half][:, first:last],
-                affine[:, t, 0:1],
-                affine[:, t, 2:3],
-                ALU.mult,
-                ALU.add,
-            )
-
-        def scalar_normalise(t, half, first=0, last=HALF):
+        def scalar_normalise(t):
             nc.scalar.activation(
-                z_planes[half][:, t, first:last],
-                banks[t, half][:, first:last],
-                ACT.Relu,
-                bias=affine[:, t, 2:3],
-                scale=affine[:, t, 1:2],
+                z_slots[1][:, t, :], banks[t, 1][:], ACT.Relu, bias=affine[:, t, 2:3], scale=affine[:, t, 1:2]
             )
 
-        for t, half in [[0,0],[3,0],[1,0],[0,1],[1,1],[2,0],[2,1],[3,1]]:
+        for t, half in [(0, 0), (3, 0), (1, 0), (0, 1), (1, 1), (2, 0), (2, 1), (3, 1)]:
             first_product(t, half)
-        scalar_mean(0, 0, 3)
-        scalar_mean(1, 0, 3)
+
+        scalar_mean(0)
+        scalar_mean(1)
         vector_stats(3, 0)
-        scalar_spread(0, 0, 3)
+        scalar_spread(0)
         vector_stats(0, 1)
-        scalar_spread(1, 0, 3)
+        scalar_spread(1)
         vector_stats(1, 1)
-        aggregate(0, 3, 12)
-        scalar_mean(2, 0, 3)
+        aggregate(0)
+        scalar_mean(2)
         vector_stats(2, 1)
         coefficients(0)
-        aggregate(1, 3, 12)
-        scalar_spread(2, 0, 3)
+        aggregate(1)
+        scalar_spread(2)
         vector_stats(3, 1)
         coefficients(1)
-        aggregate(2, 3, 12)
-        aggregate(3, 0, 12)
-        scalar_normalise(0, 1)
-        vector_normalise(0, 0)
+        aggregate(2)
+        aggregate(3)
+        scalar_normalise(0)
+        vector_normalise(0)
         coefficients(2)
         coefficients(3)
-        scalar_normalise(1, 1)
-        vector_normalise(1, 0)
-        vector_normalise(3, 0)
-        vector_normalise(2, 0)
-        scalar_normalise(2, 1)
-        scalar_normalise(3, 1)
+        scalar_normalise(1)
+        vector_normalise(1)
+        vector_normalise(3)
+        vector_normalise(2)
+        scalar_normalise(2)
+        scalar_normalise(3)
 
         out_view = out.rearrange("(a p) n -> p a n", p=P)
         woven = {}
@@ -229,7 +210,7 @@ def tile_picked_inorm_relu_p_kernel(
             half, first = divmod(start, HALF)
             z_bf = keep.tile([P, width * PACK], BF16, name="z_bf%d" % start, align_bytes=64)
             dst = z_bf[:].rearrange("p (g i t) -> p g t i", i=4, t=PACK)
-            src = z_planes[half][:, :, first : first + width].rearrange("p t (g i) -> p g t i", i=4)
+            src = z_slots[half][:, :, first : first + width].rearrange("p t (g i) -> p g t i", i=4)
             if on_scalar:
                 nc.scalar.copy(dst, src)
             elif half == 0:
@@ -255,37 +236,38 @@ def tile_picked_inorm_relu_p_kernel(
                 )
             products[start] = bank
 
-        def empty(start, width, on_scalar, store_start, store_width):
-            if store_start not in results:
-                results[store_start] = keep.tile([P, 2, store_width], F32, name="result%d" % store_start)
-            dst = results[store_start][:, :, start - store_start : start - store_start + width]
+        def empty(start, width, on_scalar):
+            first = start % WIDE
+            if start - first not in results:
+                results[start - first] = keep.tile([P, 2, WIDE], F32, name="result%d" % (start - first))
+            dst = results[start - first][:, :, first : first + width]
             if on_scalar:
                 nc.scalar.copy(dst, products[start][:])
             else:
                 nc.vector.tensor_copy(dst, products[start][:])
 
-        def store(start, width):
-            nc.sync.dma_start(out_view[:, :, start : start + width], results[start][:])
+        def store(start):
+            nc.sync.dma_start(out_view[:, :, start : start + WIDE], results[start][:])
 
-        weave(0, 256, False)
-        weave(768, 256, True)
-        weave(256, 128, False)
-        second_product(0, 256, "bank00")
-        empty(0, 256, True, 0, 256)
-        store(0, 256)
-        weave(384, 128, False)
-        second_product(256, 128, "bank10")
-        second_product(768, 256, "bank20")
-        weave(512, 128, False)
-        second_product(384, 128, "bank30")
-        empty(256, 128, True, 256, 256)
-        empty(768, 256, True, 768, 256)
-        store(768, 256)
-        empty(384, 128, True, 256, 256)
-        store(256, 256)
-        weave(640, 128, False)
-        second_product(512, 128, "bank01")
-        second_product(640, 128, "bank11")
-        empty(512, 128, False, 512, 256)
-        empty(640, 128, False, 512, 256)
-        store(512, 256)
+        weave(0, WIDE, False)
+        weave(3 * WIDE, WIDE, True)
+        weave(WIDE, NARROW, False)
+        second_product(0, WIDE, "bank00")
+        empty(0, WIDE, True)
+        store(0)
+        weave(WIDE + NARROW, NARROW, False)
+        second_product(WIDE, NARROW, "bank10")
+        second_product(3 * WIDE, WIDE, "bank20")
+        weave(2 * WIDE, NARROW, False)
+        second_product(WIDE + NARROW, NARROW, "bank30")
+        empty(WIDE, NARROW, True)
+        empty(3 * WIDE, WIDE, True)
+        store(3 * WIDE)
+        empty(WIDE + NARROW, NARROW, True)
+        store(WIDE)
+        weave(2 * WIDE + NARROW, NARROW, False)
+        second_product(2 * WIDE, NARROW, "bank01")
+        second_product(2 * WIDE + NARROW, NARROW, "bank11")
+        empty(2 * WIDE, NARROW, False)
+        empty(2 * WIDE + NARROW, NARROW, False)
+        store(2 * WIDE)

@@ -95,7 +95,7 @@ def tile_picked_inorm_relu_p_kernel(
         neg_gam = keep.tile([P, PACK], F32, name="neg_gam")
         nc.vector.tensor_scalar(neg_gam[:], gam[:], -1.0, None, ALU.mult)
 
-        idle = psum.tile([32, H], F32, name="bank31")
+        idle = psum.tile([32, H], F32, name="bank21")
         for step in range(2):
             nc.tensor.matmul_mx(
                 out=idle[:],
@@ -152,7 +152,9 @@ def tile_picked_inorm_relu_p_kernel(
         def aggregate(t):
             first = 3 if t in SCALAR_SLOTS else 0
             nc.vector.bn_aggr(moments[:, t, 2:4], stats[:, t, first:12])
-            nc.scalar.activation(rstd[:, t : t + 1], moments[:, t, 3:4], ACT.Abs_reciprocal_sqrt, bias=EPS)
+
+        def inverse_root(slots):
+            nc.scalar.activation(rstd[:, slots], moments[:, slots, 3], ACT.Abs_reciprocal_sqrt, bias=EPS)
 
         def coefficients(t):
             nc.vector.tensor_scalar(
@@ -170,7 +172,7 @@ def tile_picked_inorm_relu_p_kernel(
                 z_slots[1][:, t, :], banks[t, 1][:], ACT.Relu, bias=affine[:, t, 2:3], scale=affine[:, t, 1:2]
             )
 
-        for t, half in [(0, 0), (3, 0), (1, 0), (0, 1), (1, 1), (2, 0), (2, 1), (3, 1)]:
+        for t, half in [(0, 0), (3, 0), (1, 0), (0, 1), (1, 1), (2, 0), (3, 1), (2, 1)]:
             first_product(t, half)
 
         scalar_mean(0)
@@ -182,24 +184,27 @@ def tile_picked_inorm_relu_p_kernel(
         vector_stats(1, 1)
         aggregate(0)
         scalar_mean(2)
-        vector_stats(2, 1)
-        coefficients(0)
+        inverse_root(slice(0, 1))
+        vector_stats(3, 1)
         aggregate(1)
         scalar_spread(2)
-        vector_stats(3, 1)
-        coefficients(1)
-        aggregate(2)
+        vector_stats(2, 1)
         aggregate(3)
+        inverse_root(slice(1, 4, 2))
+        coefficients(0)
+        aggregate(2)
         scalar_normalise(0)
+        inverse_root(slice(2, 3))
         vector_normalise(0)
-        coefficients(2)
+        coefficients(1)
         coefficients(3)
-        scalar_normalise(1)
         vector_normalise(1)
+        coefficients(2)
+        scalar_normalise(1)
         vector_normalise(3)
         vector_normalise(2)
-        scalar_normalise(2)
         scalar_normalise(3)
+        scalar_normalise(2)
 
         out_view = out.rearrange("(a p) n -> p a n", p=P)
         woven = {}

@@ -172,7 +172,7 @@ def tile_picked_inorm_relu_p_kernel(
                 z_slots[1][:, t, :], banks[t, 1][:], ACT.Relu, bias=affine[:, t, 2:3], scale=affine[:, t, 1:2]
             )
 
-        for t, half in [(0, 0), (3, 0), (1, 0), (0, 1), (1, 1), (2, 0), (3, 1), (2, 1)]:
+        for t, half in [(0, 0), (1, 0), (3, 0), (0, 1), (1, 1), (2, 0), (3, 1), (2, 1)]:
             first_product(t, half)
 
         scalar_mean(0)
@@ -187,11 +187,11 @@ def tile_picked_inorm_relu_p_kernel(
         inverse_root(slice(0, 1))
         vector_stats(3, 1)
         aggregate(1)
+        coefficients(0)
         scalar_spread(2)
         vector_stats(2, 1)
         aggregate(3)
         inverse_root(slice(1, 4, 2))
-        coefficients(0)
         aggregate(2)
         scalar_normalise(0)
         inverse_root(slice(2, 3))
@@ -272,7 +272,22 @@ def tile_picked_inorm_relu_p_kernel(
         store(WIDE)
         weave(2 * WIDE + NARROW, NARROW, False)
         second_product(2 * WIDE, NARROW, "bank01")
-        second_product(2 * WIDE + NARROW, NARROW, "bank11")
+        last = 2 * WIDE + NARROW
+        z_codes = keep.tile([P, NARROW], U32, name="z_codes_last", align_bytes=64)
+        z_plane = keep.tile([P, NARROW], U8, name="z_plane_last", align_bytes=64)
+        nc.vector.quantize_mx(out=z_codes[:].bitcast(FP8X4), scales=z_plane[:], in_=woven[last][:])
+        rows = [psum.tile([P, NARROW], F32, name=name) for name in ("bank11", "bank31")]
+        for a in range(2):
+            nc.tensor.matmul_mx(
+                out=rows[a][:],
+                lhsT=w2_codes[:, 2 * P * a : 2 * P * (a + 1)].bitcast(FP4X4),
+                lhsT_scale=w2_plane[:, P * a : P * (a + 1)],
+                rhs=z_codes[:].bitcast(FP8X4),
+                rhs_scale=z_plane[:],
+                start=True,
+                stop=True,
+            )
         empty(2 * WIDE, NARROW, False)
-        empty(2 * WIDE + NARROW, NARROW, False)
+        nc.scalar.copy(results[2 * WIDE][:, 0, NARROW:WIDE], rows[0][:])
+        nc.vector.tensor_copy(results[2 * WIDE][:, 1, NARROW:WIDE], rows[1][:])
         store(2 * WIDE)

@@ -143,7 +143,12 @@ def tile_picked_inorm_relu_p_kernel(
 
         def scalar_spread(t):
             nc.scalar.activation(
-                squares[:], banks[t, 0][:], ACT.Square, bias=stats[:, t, 4:5], scale=-1.0, accum_out=stats[:, t, 5:6]
+                squares[:],
+                shrunk[t][:],
+                ACT.Square,
+                bias=stats[:, t, 4:5],
+                scale=-float(HALF),
+                accum_out=stats[:, t, 5:6],
             )
 
         def vector_stats(t, half):
@@ -172,7 +177,7 @@ def tile_picked_inorm_relu_p_kernel(
                 z_slots[1][:, t, :], banks[t, 1][:], ACT.Relu, bias=affine[:, t, 2:3], scale=affine[:, t, 1:2]
             )
 
-        for t, half in [(0, 0), (1, 0), (3, 0), (0, 1), (1, 1), (2, 0), (3, 1), (2, 1)]:
+        for t, half in [(0, 0), (3, 0), (1, 0), (0, 1), (1, 1), (2, 0), (3, 1), (2, 1)]:
             first_product(t, half)
 
         scalar_mean(0)

@@ -23,7 +23,7 @@ QUADRANTS = 4
 HALF = 512
 WIDE = 256
 NARROW = 128
-VECTOR_SHARE = 84
+VECTOR_SHARE = 96
 SCALAR_SLOTS = (0, 1, 2)
 
 
@@ -47,8 +47,8 @@ def tile_picked_inorm_relu_p_kernel(
         nc.sync.dma_start(scale_table[:].bitcast(I32)[4:P:8, :], x_scales[0].bitcast(I32))
         word_table = keep.tile([P, T], U32, name="word_table", align_bytes=64)
         x_flat = x_words[0].rearrange("p n t -> p (n t)").bitcast(I32)
-        nc.sync.dma_start(word_table[:].bitcast(I32)[:, 0 : T // 2], x_flat[:, 0 : T // 2])
         nc.sync.dma_start(w1_raw[:, 2:4, :], w1_rows[:, 2:4, :])
+        nc.sync.dma_start(word_table[:].bitcast(I32)[:, 0 : T // 2], x_flat[:, 0 : T // 2])
         nc.sync.dma_start(word_table[:].bitcast(I32)[:, T // 2 : T], x_flat[:, T // 2 : T])
         w2_codes = keep.tile([P, 2 * N], U8, name="w2_codes", align_bytes=64)
         nc.sync.dma_start(w2_codes[:].bitcast(I32), w2_words[0].bitcast(I32))

@@ -95,17 +95,20 @@ def tile_picked_inorm_relu_p_kernel(
         neg_gam = keep.tile([P, PACK], F32, name="neg_gam")
         nc.vector.tensor_scalar(neg_gam[:], gam[:], -1.0, None, ALU.mult)
 
-        idle = psum.tile([32, H], F32, name="bank21")
-        for step in range(2):
-            nc.tensor.matmul_mx(
-                out=idle[:],
-                lhsT=w1_codes[:, 0:32].bitcast(FP8X4),
-                lhsT_scale=w1_plane[:, 0:32],
-                rhs=w1_codes[:].bitcast(FP8X4),
-                rhs_scale=w1_plane[:],
-                start=True,
-                stop=True,
-            )
+        def warm_up(bank_name):
+            idle = psum.tile([32, H], F32, name=bank_name)
+            for step in range(2):
+                nc.tensor.matmul_mx(
+                    out=idle[:],
+                    lhsT=w1_codes[:, 0:32].bitcast(FP8X4),
+                    lhsT_scale=w1_plane[:, 0:32],
+                    rhs=w1_codes[:].bitcast(FP8X4),
+                    rhs_scale=w1_plane[:],
+                    start=True,
+                    stop=True,
+                )
+
+        warm_up("bank21")
 
         picked_words = []
         for half in range(2):
@@ -199,6 +202,7 @@ def tile_picked_inorm_relu_p_kernel(
         inverse_root(slice(1, 4, 2))
         aggregate(2)
         scalar_normalise(0)
+        warm_up("bank01")
         inverse_root(slice(2, 3))
         vector_normalise(0)
         coefficients(1)

@@ -223,8 +223,8 @@ def tile_picked_inorm_relu_p_kernel(
         def weave(start, width, on_scalar):
             half, first = divmod(start, HALF)
             z_bf = keep.tile([P, width * PACK], BF16, name="z_bf%d" % start, align_bytes=64)
-            dst = z_bf[:].rearrange("p (g i t) -> p g t i", i=4, t=PACK)
-            src = z_slots[half][:, :, first : first + width].rearrange("p t (g i) -> p g t i", i=4)
+            dst = z_bf[:].rearrange("p (g i t) -> p g t i", i=2, t=PACK)
+            src = z_slots[half][:, :, first : first + width].rearrange("p t (g i) -> p g t i", i=2)
             if on_scalar:
                 nc.scalar.copy(dst, src)
             elif half == 0:

@@ -141,7 +141,7 @@ def tile_picked_inorm_relu_p_kernel(
 
         def scalar_mean(t):
             h_small = keep.tile([P, HALF], F32, name="h_small%d" % t)
-            nc.scalar.activation(h_small[:], banks[t, 0][:], ACT.Identity, scale=1.0 / HALF, accum_out=stats[:, t, 4:5])
+            nc.scalar.activation(h_small[:], banks[t, 0][:], ACT.Copy, scale=1.0 / HALF, accum_out=stats[:, t, 4:5])
             shrunk[t] = h_small
 
         def scalar_spread(t):

@@ -95,20 +95,20 @@ def tile_picked_inorm_relu_p_kernel(
         neg_gam = keep.tile([P, PACK], F32, name="neg_gam")
         nc.vector.tensor_scalar(neg_gam[:], gam[:], -1.0, None, ALU.mult)
 
-        def warm_up(bank_name):
-            idle = psum.tile([32, H], F32, name=bank_name)
+        def warm_up(bank_name, width):
+            idle = psum.tile([32, width], F32, name=bank_name)
             for step in range(2):
                 nc.tensor.matmul_mx(
                     out=idle[:],
                     lhsT=w1_codes[:, 0:32].bitcast(FP8X4),
                     lhsT_scale=w1_plane[:, 0:32],
-                    rhs=w1_codes[:].bitcast(FP8X4),
-                    rhs_scale=w1_plane[:],
+                    rhs=w1_codes[:, 0:width].bitcast(FP8X4),
+                    rhs_scale=w1_plane[:, 0:width],
                     start=True,
                     stop=True,
                 )
 
-        warm_up("bank21")
+        warm_up("bank21", H)
 
         picked_words = []
         for half in range(2):
@@ -202,7 +202,7 @@ def tile_picked_inorm_relu_p_kernel(
         inverse_root(slice(1, 4, 2))
         aggregate(2)
         scalar_normalise(0)
-        warm_up("bank01")
+        warm_up("bank01", H)
         inverse_root(slice(2, 3))
         vector_normalise(0)
         coefficients(1)
@@ -214,6 +214,7 @@ def tile_picked_inorm_relu_p_kernel(
         vector_normalise(2)
         scalar_normalise(3)
         scalar_normalise(2)
+        warm_up("bank21", NARROW)
 
         out_view = out.rearrange("(a p) n -> p a n", p=P)
         woven = {}

@@ -202,7 +202,6 @@ def tile_picked_inorm_relu_p_kernel(
         inverse_root(slice(1, 4, 2))
         aggregate(2)
         scalar_normalise(0)
-        warm_up("bank01", H)
         inverse_root(slice(2, 3))
         vector_normalise(0)
         coefficients(1)
@@ -210,6 +209,7 @@ def tile_picked_inorm_relu_p_kernel(
         vector_normalise(1)
         coefficients(2)
         scalar_normalise(1)
+        warm_up("bank11", H)
         vector_normalise(3)
         vector_normalise(2)
         scalar_normalise(3)
@@ -251,6 +251,33 @@ def tile_picked_inorm_relu_p_kernel(
                 )
             products[start] = bank
 
+        def second_product_by_rows(start, width, bank_names):
+            z_codes = keep.tile([P, width], U32, name="z_codes%d" % start, align_bytes=64)
+            z_plane = keep.tile([P, width], U8, name="z_plane%d" % start, align_bytes=64)
+            nc.vector.quantize_mx(out=z_codes[:].bitcast(FP8X4), scales=z_plane[:], in_=woven[start][:])
+            rows = [psum.tile([P, width], F32, name=name) for name in bank_names]
+            for a in range(2):
+                nc.tensor.matmul_mx(
+                    out=rows[a][:],
+                    lhsT=w2_codes[:, 2 * P * a : 2 * P * (a + 1)].bitcast(FP4X4),
+                    lhsT_scale=w2_plane[:, P * a : P * (a + 1)],
+                    rhs=z_codes[:].bitcast(FP8X4),
+                    rhs_scale=z_plane[:],
+                    start=True,
+                    stop=True,
+                )
+            products[start] = rows
+
+        def empty_rows(start, width, a, on_scalar):
+            first = start % WIDE
+            if start - first not in results:
+                results[start - first] = keep.tile([P, 2, WIDE], F32, name="result%d" % (start - first))
+            dst = results[start - first][:, a, first : first + width]
+            if on_scalar:
+                nc.scalar.copy(dst, products[start][a][:])
+            else:
+                nc.vector.tensor_copy(dst, products[start][a][:])
+
         def empty(start, width, on_scalar):
             first = start % WIDE
             if start - first not in results:
@@ -267,37 +294,25 @@ def tile_picked_inorm_relu_p_kernel(
         weave(0, WIDE, False)
         weave(3 * WIDE, WIDE, True)
         weave(WIDE, NARROW, False)
-        second_product(0, WIDE, "bank00")
-        empty(0, WIDE, True)
+        second_product_by_rows(0, WIDE, ("bank00", "bank10"))
+        empty_rows(0, WIDE, 0, True)
+        empty_rows(0, WIDE, 1, True)
         store(0)
         weave(WIDE + NARROW, NARROW, False)
-        second_product(WIDE, NARROW, "bank10")
-        second_product(3 * WIDE, WIDE, "bank20")
+        second_product(WIDE, NARROW, "bank01")
+        second_product_by_rows(3 * WIDE, WIDE, ("bank20", "bank21"))
         weave(2 * WIDE, NARROW, False)
         second_product(WIDE + NARROW, NARROW, "bank30")
         empty(WIDE, NARROW, True)
-        empty(3 * WIDE, WIDE, True)
+        empty_rows(3 * WIDE, WIDE, 0, True)
+        empty_rows(3 * WIDE, WIDE, 1, True)
         store(3 * WIDE)
         empty(WIDE + NARROW, NARROW, True)
         store(WIDE)
         weave(2 * WIDE + NARROW, NARROW, False)
-        second_product(2 * WIDE, NARROW, "bank01")
-        last = 2 * WIDE + NARROW
-        z_codes = keep.tile([P, NARROW], U32, name="z_codes_last", align_bytes=64)
-        z_plane = keep.tile([P, NARROW], U8, name="z_plane_last", align_bytes=64)
-        nc.vector.quantize_mx(out=z_codes[:].bitcast(FP8X4), scales=z_plane[:], in_=woven[last][:])
-        rows = [psum.tile([P, NARROW], F32, name=name) for name in ("bank11", "bank31")]
-        for a in range(2):
-            nc.tensor.matmul_mx(
-                out=rows[a][:],
-                lhsT=w2_codes[:, 2 * P * a : 2 * P * (a + 1)].bitcast(FP4X4),
-                lhsT_scale=w2_plane[:, P * a : P * (a + 1)],
-                rhs=z_codes[:].bitcast(FP8X4),
-                rhs_scale=z_plane[:],
-                start=True,
-                stop=True,
-            )
+        second_product(2 * WIDE, NARROW, "bank00")
+        second_product_by_rows(2 * WIDE + NARROW, NARROW, ("bank11", "bank31"))
         empty(2 * WIDE, NARROW, False)
-        nc.scalar.copy(results[2 * WIDE][:, 0, NARROW:WIDE], rows[0][:])
-        nc.vector.tensor_copy(results[2 * WIDE][:, 1, NARROW:WIDE], rows[1][:])
+        empty_rows(2 * WIDE + NARROW, NARROW, 0, True)
+        empty_rows(2 * WIDE + NARROW, NARROW, 1, False)
         store(2 * WIDE)

from contextlib import ExitStack

import concourse.mybir as mybir

K, T, S, H, N = 512, 4096, 1024, 512, 256
FLOPS = 2 * K * H * S + 2 * H * N * S
EPS = 1e-5

F32 = mybir.dt.float32
BF16 = mybir.dt.bfloat16
I32 = mybir.dt.int32
U32 = mybir.dt.uint32
U16 = mybir.dt.uint16
U8 = mybir.dt.uint8
FP8X4 = mybir.dt.float8_e4m3fn_x4
FP4X4 = mybir.dt.float4_e2m1fn_x4
ACT = mybir.ActivationFunctionType
ALU = mybir.AluOpType

P = 128
PACK = 4
QUADRANTS = 4
HALF = 512
WIDE = 256
NARROW = 128
VECTOR_SHARE = 96
SCALAR_SLOTS = (0, 1, 2)


def tile_picked_inorm_relu_p_kernel(
    tc, x_words, x_scales, w1, w2_words, w2_scales, gamma, offs, out
):
    nc = tc.nc
    with ExitStack() as ctx:
        keep = ctx.enter_context(tc.tile_pool(name="keep", bufs=1))
        psum = ctx.enter_context(tc.psum_pool(name="psum", bufs=1))

        offsets = keep.tile([P, S // 16], U16, name="offsets")
        w1_raw = keep.tile([P, PACK, H], F32, name="w1_raw")
        w1_rows = w1.rearrange("(p j) c -> p j c", j=PACK)
        nc.sync.dma_start(w1_raw[:, 0:2, :], w1_rows[:, 0:2, :])
        nc.sync.dma_start(offsets[:], offs)
        gam = keep.tile([P, PACK], F32, name="gam")
        nc.sync.dma_start(gam[:], gamma.rearrange("(p t) o -> p (t o)", t=PACK))
        scale_table = keep.tile([P, T], U8, name="scale_table", align_bytes=64)
        nc.vector.memset(scale_table[:].bitcast(I32), 0)
        nc.sync.dma_start(scale_table[:].bitcast(I32)[4:P:8, :], x_scales[0].bitcast(I32))
        word_table = keep.tile([P, T], U32, name="word_table", align_bytes=64)
        x_flat = x_words[0].rearrange("p n t -> p (n t)").bitcast(I32)
        nc.sync.dma_start(w1_raw[:, 2:4, :], w1_rows[:, 2:4, :])
        nc.sync.dma_start(word_table[:].bitcast(I32)[:, 0 : T // 2], x_flat[:, 0 : T // 2])
        nc.sync.dma_start(word_table[:].bitcast(I32)[:, T // 2 : T], x_flat[:, T // 2 : T])
        w2_codes = keep.tile([P, 2 * N], U8, name="w2_codes", align_bytes=64)
        nc.sync.dma_start(w2_codes[:].bitcast(I32), w2_words[0].bitcast(I32))

        warm = keep.tile([P, 2], F32, name="warm")
        nc.vector.memset(warm[:, 0:1], 1.0)
        nc.scalar.activation(warm[:, 1:2], warm[:, 0:1], ACT.Abs_reciprocal_sqrt)

        w2_plane = keep.tile([P, N], U8, name="w2_plane", align_bytes=64)
        nc.vector.memset(w2_plane[:].bitcast(I32), 0)
        for q in range(QUADRANTS):
            nc.gpsimd.dma_start(
                w2_plane[:].bitcast(I32)[32 * q : 32 * q + 4, :], w2_scales[0].bitcast(I32)[4 * q : 4 * q + 4, :]
            )

        x_plane = keep.tile([P, S], U8, name="x_plane", align_bytes=64)
        nc.vector.memset(x_plane[:].bitcast(I32), 0)
        stats = keep.tile([P, PACK, 12], F32, name="stats")
        nc.vector.memset(stats[:], float(HALF))
        moments = keep.tile([P, PACK, 4], F32, name="moments")
        nc.vector.memset(moments[:, :, 0:1], -float(HALF))
        nc.vector.memset(moments[:, :, 1:2], -1.0)

        picked_scales = keep.tile([P, S], U8, name="picked_scales", align_bytes=64)
        nc.vector.tensor_copy(picked_scales[:], scale_table[:].indirect(offsets[:]))

        w1_bf = keep.tile([P, PACK * H], BF16, name="w1_bf", align_bytes=64)
        w1_dst = w1_bf[:].rearrange("p (u e m j) -> p u m j e", u=2, e=2, j=PACK)
        w1_src = w1_raw[:].rearrange("p j (m u e) -> p u m j e", u=2, e=2)
        nc.scalar.copy(w1_dst[:, :, :, 0:2], w1_src[:, :, :, 0:2])
        nc.vector.tensor_copy(w1_dst[:, :, 0:VECTOR_SHARE, 2:4], w1_src[:, :, 0:VECTOR_SHARE, 2:4])
        nc.scalar.copy(w1_dst[:, :, VECTOR_SHARE:P, 2:4], w1_src[:, :, VECTOR_SHARE:P, 2:4])

        for q in range(QUADRANTS):
            nc.scalar.dma_start(
                x_plane[:].bitcast(I32)[32 * q : 32 * q + 4, :],
                picked_scales[:].bitcast(I32)[32 * q + 4 : 32 * q + 32 : 8, :],
            )

        w1_codes = keep.tile([P, H], U32, name="w1_codes", align_bytes=64)
        w1_plane = keep.tile([P, H], U8, name="w1_plane", align_bytes=64)
        nc.vector.quantize_mx(out=w1_codes[:].bitcast(FP8X4), scales=w1_plane[:], in_=w1_bf[:])

        neg_gam = keep.tile([P, PACK], F32, name="neg_gam")
        nc.vector.tensor_scalar(neg_gam[:], gam[:], -1.0, None, ALU.mult)

        def warm_up(bank_name, width):
            idle = psum.tile([32, width], F32, name=bank_name)
            for step in range(2):
                nc.tensor.matmul_mx(
                    out=idle[:],
                    lhsT=w1_codes[:, 0:32].bitcast(FP8X4),
                    lhsT_scale=w1_plane[:, 0:32],
                    rhs=w1_codes[:, 0:width].bitcast(FP8X4),
                    rhs_scale=w1_plane[:, 0:width],
                    start=True,
                    stop=True,
                )

        warm_up("bank21", H)

        picked_words = []
        for half in range(2):
            words = keep.tile([P, HALF], U32, name="picked_words%d" % half, align_bytes=64)
            cols = slice(half * HALF // 16, (half + 1) * HALF // 16)
            nc.vector.tensor_copy(words[:], word_table[:].indirect(offsets[:, cols]))
            picked_words.append(words)

        rstd = keep.tile([P, PACK], F32, name="rstd")
        affine = keep.tile([P, PACK, 4], F32, name="affine")
        z_slots = [keep.tile([P, PACK, HALF], BF16, name="z_slots%d" % half, align_bytes=64) for half in range(2)]
        squares = keep.tile([P, HALF], BF16, name="squares")

        banks = {}
        shrunk = {}

        def first_product(t, half):
            bank = psum.tile([P, HALF], F32, name="bank%d%d" % (t, half))
            cols = slice(t * P, (t + 1) * P)
            nc.tensor.matmul_mx(
                out=bank[:],
                lhsT=w1_codes[:, cols].bitcast(FP8X4),
                lhsT_scale=w1_plane[:, cols],
                rhs=picked_words[half][:].bitcast(FP8X4),
                rhs_scale=x_plane[:, half * HALF : (half + 1) * HALF],
                start=True,
                stop=True,
            )
            banks[t, half] = bank

        def scalar_mean(t):
            h_small = keep.tile([P, HALF], F32, name="h_small%d" % t)
            nc.scalar.activation(h_small[:], banks[t, 0][:], ACT.Copy, scale=1.0 / HALF, accum_out=stats[:, t, 4:5])
            shrunk[t] = h_small

        def scalar_spread(t):
            nc.scalar.activation(
                squares[:],
                shrunk[t][:],
                ACT.Square,
                bias=stats[:, t, 4:5],
                scale=-float(HALF),
                accum_out=stats[:, t, 5:6],
            )

        def vector_stats(t, half):
            nc.vector.bn_stats(stats[:, t, 6 * half : 6 * half + 6], banks[t, half][:])

        def aggregate(t):
            first = 3 if t in SCALAR_SLOTS else 0
            nc.vector.bn_aggr(moments[:, t, 2:4], stats[:, t, first:12])

        def inverse_root(slots):
            nc.scalar.activation(rstd[:, slots], moments[:, slots, 3], ACT.Abs_reciprocal_sqrt, bias=EPS)

        def coefficients(t):
            nc.vector.tensor_scalar(
                affine[:, t, 0:3], moments[:, t, 0:3], rstd[:, t : t + 1], neg_gam[:, t : t + 1], ALU.mult, ALU.mult
            )

        def vector_normalise(t):
            source, column = (shrunk[t], 0) if t in SCALAR_SLOTS else (banks[t, 0], 1)
            nc.vector.tensor_scalar(
                z_slots[0][:, t, :], source[:], affine[:, t, column : column + 1], affine[:, t, 2:3], ALU.mult, ALU.add
            )

        def scalar_normalise(t):
            nc.scalar.activation(
                z_slots[1][:, t, :], banks[t, 1][:], ACT.Relu, bias=affine[:, t, 2:3], scale=affine[:, t, 1:2]
            )

        for t, half in [(0, 0), (3, 0), (1, 0), (0, 1), (1, 1), (2, 0), (3, 1), (2, 1)]:
            first_product(t, half)

        scalar_mean(0)
        scalar_mean(1)
        vector_stats(3, 0)
        scalar_spread(0)
        vector_stats(0, 1)
        scalar_spread(1)
        vector_stats(1, 1)
        aggregate(0)
        scalar_mean(2)
        inverse_root(slice(0, 1))
        vector_stats(3, 1)
        aggregate(1)
        coefficients(0)
        scalar_spread(2)
        vector_stats(2, 1)
        aggregate(3)
        inverse_root(slice(1, 4, 2))
        aggregate(2)
        scalar_normalise(0)
        inverse_root(slice(2, 3))
        vector_normalise(0)
        coefficients(1)
        coefficients(3)
        vector_normalise(1)
        coefficients(2)
        scalar_normalise(1)
        warm_up("bank11", H)
        vector_normalise(3)
        vector_normalise(2)
        scalar_normalise(3)
        scalar_normalise(2)
        warm_up("bank21", NARROW)

        out_view = out.rearrange("(a p) n -> p a n", p=P)
        woven = {}
        products = {}
        results = {}

        def weave(start, width, on_scalar):
            half, first = divmod(start, HALF)
            z_bf = keep.tile([P, width * PACK], BF16, name="z_bf%d" % start, align_bytes=64)
            dst = z_bf[:].rearrange("p (g i t) -> p g t i", i=2, t=PACK)
            src = z_slots[half][:, :, first : first + width].rearrange("p t (g i) -> p g t i", i=2)
            if on_scalar:
                nc.scalar.copy(dst, src)
            elif half == 0:
                nc.vector.tensor_scalar(dst, src, 0.0, None, ALU.max)
            else:
                nc.vector.tensor_copy(dst, src)
            woven[start] = z_bf

        def second_product(start, width, bank_name):
            z_codes = keep.tile([P, width], U32, name="z_codes%d" % start, align_bytes=64)
            z_plane = keep.tile([P, width], U8, name="z_plane%d" % start, align_bytes=64)
            nc.vector.quantize_mx(out=z_codes[:].bitcast(FP8X4), scales=z_plane[:], in_=woven[start][:])
            bank = psum.tile([P, 2, width], F32, name=bank_name)
            for a in range(2):
                nc.tensor.matmul_mx(
                    out=bank[:, a, :],
                    lhsT=w2_codes[:, 2 * P * a : 2 * P * (a + 1)].bitcast(FP4X4),
                    lhsT_scale=w2_plane[:, P * a : P * (a + 1)],
                    rhs=z_codes[:].bitcast(FP8X4),
                    rhs_scale=z_plane[:],
                    start=True,
                    stop=True,
                )
            products[start] = bank

        def second_product_by_rows(start, width, bank_names):
            z_codes = keep.tile([P, width], U32, name="z_codes%d" % start, align_bytes=64)
            z_plane = keep.tile([P, width], U8, name="z_plane%d" % start, align_bytes=64)
            nc.vector.quantize_mx(out=z_codes[:].bitcast(FP8X4), scales=z_plane[:], in_=woven[start][:])
            rows = [psum.tile([P, width], F32, name=name) for name in bank_names]
            for a in range(2):
                nc.tensor.matmul_mx(
                    out=rows[a][:],
                    lhsT=w2_codes[:, 2 * P * a : 2 * P * (a + 1)].bitcast(FP4X4),
                    lhsT_scale=w2_plane[:, P * a : P * (a + 1)],
                    rhs=z_codes[:].bitcast(FP8X4),
                    rhs_scale=z_plane[:],
                    start=True,
                    stop=True,
                )
            products[start] = rows

        def empty_rows(start, width, a, on_scalar):
            first = start % WIDE
            if start - first not in results:
                results[start - first] = keep.tile([P, 2, WIDE], F32, name="result%d" % (start - first))
            dst = results[start - first][:, a, first : first + width]
            if on_scalar:
                nc.scalar.copy(dst, products[start][a][:])
            else:
                nc.vector.tensor_copy(dst, products[start][a][:])

        def empty(start, width, on_scalar):
            first = start % WIDE
            if start - first not in results:
                results[start - first] = keep.tile([P, 2, WIDE], F32, name="result%d" % (start - first))
            dst = results[start - first][:, :, first : first + width]
            if on_scalar:
                nc.scalar.copy(dst, products[start][:])
            else:
                nc.vector.tensor_copy(dst, products[start][:])

        def store(start):
            nc.sync.dma_start(out_view[:, :, start : start + WIDE], results[start][:])

        weave(0, WIDE, False)
        weave(3 * WIDE, WIDE, True)
        weave(WIDE, NARROW, False)
        second_product_by_rows(0, WIDE, ("bank00", "bank10"))
        empty_rows(0, WIDE, 0, True)
        empty_rows(0, WIDE, 1, True)
        store(0)
        weave(WIDE + NARROW, NARROW, False)
        second_product(WIDE, NARROW, "bank01")
        second_product_by_rows(3 * WIDE, WIDE, ("bank20", "bank21"))
        weave(2 * WIDE, NARROW, False)
        second_product(WIDE + NARROW, NARROW, "bank30")
        empty(WIDE, NARROW, True)
        empty_rows(3 * WIDE, WIDE, 0, True)
        empty_rows(3 * WIDE, WIDE, 1, True)
        store(3 * WIDE)
        empty(WIDE + NARROW, NARROW, True)
        store(WIDE)
        weave(2 * WIDE + NARROW, NARROW, False)
        second_product(2 * WIDE, NARROW, "bank00")
        second_product_by_rows(2 * WIDE + NARROW, NARROW, ("bank11", "bank31"))
        empty(2 * WIDE, NARROW, False)
        empty_rows(2 * WIDE + NARROW, NARROW, 0, True)
        empty_rows(2 * WIDE + NARROW, NARROW, 1, False)
        store(2 * WIDE)
